import numpy as np
import ml_dtypes


def mxq(x, axis, fmt="e4m3"):
    dtype, down = {"e4m3": (ml_dtypes.float8_e4m3fn, 7), "e5m2": (ml_dtypes.float8_e5m2, 14)}[fmt]
    v = np.moveaxis(np.asarray(x, np.float32).astype(ml_dtypes.bfloat16).astype(np.float64), axis, -1)
    blocks = v.reshape(v.shape[:-1] + (-1, 32))
    amax = np.abs(blocks).max(-1, keepdims=True)
    byte = np.maximum(np.where(amax > 0, np.frexp(amax)[1] - 1 + 127, 0) - down, 1)
    scale = np.exp2(byte - 127.0)
    codes = (blocks / scale).astype(np.float32).astype(dtype).astype(np.float64)
    return np.moveaxis((codes * scale).reshape(v.shape), -1, axis)


WIDE = False


def mx_kscale(k):
    if not WIDE:
        return np.ones(k)
    levels = np.array([10, -10, 5, -5, 0])
    if k % 512:
        return np.exp2(np.random.permutation(np.resize(levels, k // 32))).repeat(32)
    a = np.empty((k // 512, 16))
    for p in range(k // 512):
        a[p, :8] = np.random.permutation(np.resize(levels, 8))
        for g in range(8):
            far = levels[np.abs(levels - a[p, g]) >= 10]
            a[p, g + 8] = far[np.random.randint(len(far))]
    return np.exp2(a.ravel()).repeat(32)


def f64(x):
    return np.asarray(x).astype(np.float64)


def striped(idx):
    return np.tile(idx.reshape(-1, 16).T, (8, 1)).astype(np.uint16)


def unstriped(offs):
    return offs[:16].T.reshape(-1).astype(np.int64)


E2M1 = np.array([0.0, 0.5, 1.0, 1.5, 2.0, 3.0, 4.0, 6.0, -0.0, -0.5, -1.0, -1.5, -2.0, -3.0, -4.0, -6.0])


def pack_weight(w, fmt):
    k, n = w.shape
    w = f64(np.asarray(w, np.float32).astype(ml_dtypes.bfloat16)).reshape(k // 32, 32, n)
    amax = np.abs(w).max(1)
    if fmt == "e4m3":
        byte = np.frexp(amax)[1] - 1 + 127 - 7
    else:
        mant, ex = np.frexp(amax / 6.0)
        byte = np.where(mant > 0.5, ex, ex - 1) + 127
    byte = np.clip(np.where(amax > 0, byte, 1), 1, 254)
    scaled = (w * np.exp2(127.0 - byte)[:, None, :]).reshape(k, n).astype(np.float32)
    by_word = np.ascontiguousarray(scaled.reshape(k // 512, 128, 4, n).transpose(0, 1, 3, 2))
    if fmt == "e4m3":
        words = by_word.astype(ml_dtypes.float8_e4m3fn).view(np.uint8)
    else:
        c = by_word.astype(ml_dtypes.float4_e2m1fn).view(np.uint8) & 0xF
        words = (c[..., 0::2] | (c[..., 1::2] << 4)).reshape(k // 512, 128, 2 * n)
    return np.ascontiguousarray(words), np.ascontiguousarray(byte.astype(np.uint8).reshape(k // 512, 16, n))


def unpack_weight(words, scales, fmt):
    g, _, n = scales.shape
    words = np.ascontiguousarray(words).reshape(g, 128, n, -1)
    if fmt == "e4m3":
        vals = words.view(ml_dtypes.float8_e4m3fn).astype(np.float64)
    else:
        nib = np.empty((g, 128, n, 4), np.uint8)
        nib[..., 0::2] = words & 0xF
        nib[..., 1::2] = words >> 4
        vals = E2M1[nib]
    vals = vals * np.repeat(np.exp2(scales.astype(np.float64) - 127.0), 8, axis=1)[..., None]
    return vals.transpose(0, 1, 3, 2).reshape(g * 512, n)


def gelu(v):
    return 0.5 * v * (1.0 + np.tanh(np.sqrt(2.0 / np.pi) * (v + 0.044715 * v**3)))


K, T, S, S2 = 1024, 2048, 512, 1024

def setup_inputs():
    n = np.random.standard_normal
    s = mx_kscale(K)[:, None]
    d = {}
    d["tab_words"], d["tab_scales"] = pack_weight(n((K, T)) * s, "e4m3")
    d["offs"] = striped(np.random.permutation(T)[:S])
    d["offs2"] = striped(np.random.permutation(T)[:S2])
    d["w1"] = (0.55 * n((K, K)) / K ** 0.5 / s).astype(np.float32)
    d["w4_words"], d["w4_scales"] = pack_weight(n((K, K)) / K ** 0.5 / s, "e2m1")
    d["gain1"] = (2.0 * np.exp(0.3 * n(K)) / K ** 0.5 / s[:, 0]).astype(np.float32)
    d["gain2"] = (np.exp(0.3 * n(K)) / K ** 0.5 / s[:, 0]).astype(np.float32)
    d["bar"] = (0.5 + 0.5 * n(S2)).astype(np.float32)
    return d

def reference(tab_words, tab_scales, offs, offs2, w1, w4_words, w4_scales, gain1, gain2, bar):
    TW = unpack_weight(tab_words, tab_scales, "e4m3")
    v = TW[:, unstriped(offs)]
    v2 = TW[:, unstriped(offs2)]
    w4 = unpack_weight(w4_words, w4_scales, "e2m1")
    a1 = mxq(f64(w1), 0, "e4m3").T @ v
    h1 = np.sin(a1) * f64(gain1)[:, None]
    a2 = w4.T @ v
    h2 = a2 * f64(gain2)[:, None]
    e1 = v2.T @ mxq(h1, 0, "e4m3")
    e2 = v2.T @ mxq(h2, 0, "e4m3")
    top = np.maximum(e1, e2) - f64(bar)[:, None]
    return np.tanh(top)

@@ -1,0 +1,330 @@
+from contextlib import ExitStack
+
+import concourse.mybir as mybir
+from concourse.masks import make_identity
+
+K, T, S, S2 = 1024, 2048, 512, 1024
+FLOPS = 2 * (2 * K * K * S + 2 * K * S2 * S)
+
+F32 = mybir.dt.float32
+BF16 = mybir.dt.bfloat16
+I32 = mybir.dt.int32
+U32 = mybir.dt.uint32
+U16 = mybir.dt.uint16
+U8 = mybir.dt.uint8
+FP8X4 = mybir.dt.float8_e4m3fn_x4
+FP4X4 = mybir.dt.float4_e2m1fn_x4
+ALU = mybir.AluOpType
+ACT = mybir.ActivationFunctionType
+
+P = 128
+PACK = 4
+KP = P * PACK
+PASSES = K // KP
+QUADS = 4
+ROWS = 4
+HALF = 512
+JH = S // 2
+
+
+def tile_list_fluke_sighting_scores_kernel(
+    tc, tab_words, tab_scales, offs, offs2, w1, w4_words, w4_scales, gain1, gain2, bar, out
+):
+    nc = tc.nc
+    with ExitStack() as ctx:
+        lists = ctx.enter_context(tc.tile_pool(name="lists", bufs=1))
+        keep = ctx.enter_context(tc.tile_pool(name="keep", bufs=1))
+        ring = ctx.enter_context(tc.tile_pool(name="ring", bufs=8))
+        psum = ctx.enter_context(tc.psum_pool(name="psum", bufs=4))
+
+        def held(name, shape, dtype, tag=""):
+            return keep.tile(shape, dtype, name=name, tag=tag or name, align_bytes=64)
+
+        def bank(tag):
+            return psum.tile([P, 512], F32, name=tag)
+
+        new_list = lists.tile([P, S // 16], U16, name="new_list")
+        known_list = lists.tile([P, S2 // 16], U16, name="known_list")
+
+        tab_sc = held("tab_sc", [P, T], U8)
+        tab_sc1 = held("tab_sc1", [P, T], U8)
+        w4_sc_raw = held("w4_sc_raw", [P, PASSES * K], U8)
+        nc.vector.memset(tab_sc[:].bitcast(I32), 0)
+        nc.vector.memset(tab_sc1[:].bitcast(I32), 0)
+        bar_rows = held("bar_rows", [P, P], F32)
+        nc.gpsimd.memset(bar_rows[:], 0.0)
+        nc.gpsimd.memset(w4_sc_raw[:].bitcast(I32), 0)
+
+        def load_scales(queue, dst, src):
+            for q in range(QUADS):
+                queue.dma_start(
+                    out=dst[32 * q : 32 * q + PASSES * ROWS, :].bitcast(I32),
+                    in_=src[:, ROWS * q : ROWS * (q + 1), :].bitcast(I32),
+                )
+
+        def load_scales1():
+            for q in range(QUADS):
+                nc.sync.dma_start(
+                    out=tab_sc1[32 * q : 32 * q + ROWS, :].bitcast(I32),
+                    in_=tab_scales[1, ROWS * q : ROWS * (q + 1), :].bitcast(I32),
+                )
+
+        def load_w4_scales():
+            for q in range(QUADS):
+                nc.gpsimd.dma_start(
+                    out=w4_sc_raw[32 * q : 32 * q + ROWS, :].bitcast(I32).rearrange("r (a n) -> r a n", a=PASSES),
+                    in_=w4_scales[:, ROWS * q : ROWS * (q + 1), :].bitcast(I32).rearrange("a r n -> r a n"),
+                )
+
+        tab_w = [held("tab_w%d" % a, [P, T], U32) for a in range(PASSES)]
+        w4_raw = held("w4_raw", [P, PASSES * 2 * K], U8)
+        w1_raw = {}
+
+        def load_words(a):
+            nc.sync.dma_start(
+                out=tab_w[a][:].bitcast(I32),
+                in_=tab_words[a].rearrange("p n t -> p (n t)").bitcast(I32),
+            )
+
+        def load_w1(a, b):
+            for n in range(2):
+                w1_raw[a, b, n] = held("w1_raw%d%d%d" % (a, b, n), [P, PACK, KP // 2], F32)
+                c0 = KP * b + n * KP // 2
+                nc.sync.dma_start(
+                    out=w1_raw[a, b, n][:],
+                    in_=w1[KP * a : KP * (a + 1), c0 : c0 + KP // 2].rearrange("(p j) c -> p j c", j=PACK),
+                )
+
+        g1 = held("g1", [P, PASSES, PACK], F32)
+        g2 = held("g2", [P, PASSES, PACK], F32)
+        ident = held("ident", [P, P], F32)
+
+        nc.sync.dma_start(new_list[:], offs)
+        nc.sync.dma_start(known_list[:], offs2)
+        nc.sync.dma_start(out=g2[:], in_=gain2.rearrange("(b p t) -> p b t", p=P, t=PACK))
+        nc.sync.dma_start(out=g1[:], in_=gain1.rearrange("(b p t) -> p b t", p=P, t=PACK))
+        load_words(0)
+        nc.sync.dma_start(
+            out=w4_raw[:].bitcast(I32).rearrange("p (a n) -> p a n", a=PASSES),
+            in_=w4_words.bitcast(I32).rearrange("a p n -> p a n"),
+        )
+        load_w1(0, 0)
+        load_scales(nc.sync, tab_sc, tab_scales)
+        load_words(1)
+        nc.sync.dma_start(out=bar_rows[0 : S2 // P, :], in_=bar.rearrange("(c p) -> c p", p=P))
+        load_scales1()
+        load_w4_scales()
+        load_w1(1, 0)
+        load_w1(0, 1)
+        load_w1(1, 1)
+
+        v_sc = held("v_sc", [P, S], U8)
+        v_sc1 = held("v_sc1", [P, S], U8)
+        nc.vector.tensor_copy(v_sc[:], tab_sc[:].indirect(new_list[:]))
+        nc.vector.tensor_copy(v_sc1[:], tab_sc1[:].indirect(new_list[:]))
+
+        def known_slice(h):
+            return known_list[:, h * HALF // 16 : (h + 1) * HALF // 16]
+
+        v2_sc = {}
+
+        def gather_known_scales(h):
+            v2_sc[h] = held("v2_sc%d" % h, [P, HALF], U8, tag=("", "w1_bf00")[h])
+            nc.vector.tensor_copy(v2_sc[h][:], tab_sc[:].indirect(known_slice(h)))
+
+        w4_sc = held("w4_sc", [P, PASSES * K], U8)
+        nc.vector.tensor_copy(
+            out=w4_sc[:].rearrange("p (g t o i) -> p g o t i", g=PASSES * PASSES, t=PACK, i=16),
+            in_=w4_sc_raw[:].rearrange("p (g o i t) -> p g o t i", g=PASSES * PASSES, t=PACK, i=16),
+        )
+
+        w4_w = [held("w4_w%d" % a, [P, 2 * K], U8) for a in range(PASSES)]
+        for a in range(PASSES):
+            nc.scalar.copy(
+                out=w4_w[a][:].bitcast(U16).rearrange("p (b t o i) -> p b o t i", b=PASSES, t=PACK, i=8),
+                in_=w4_raw[:, 2 * K * a : 2 * K * (a + 1)].bitcast(U16).rearrange("p (b o i t) -> p b o t i", b=PASSES, t=PACK, i=8),
+            )
+
+        v_w = [held("v_w%d" % a, [P, S], U32) for a in range(PASSES)]
+        v2_w = {}
+
+        def gather_new(a):
+            nc.vector.tensor_copy(v_w[a][:], tab_w[a][:].indirect(new_list[:]))
+
+        def gather_known(a, h):
+            tag = {(1, 0): "w1_bf10", (1, 1): "w1_bf01"}.get((a, h), "")
+            v2_w[a, h] = held("v2_w%d%d" % (a, h), [P, HALF], U32, tag=tag)
+            nc.vector.tensor_copy(v2_w[a, h][:], tab_w[a][:].indirect(known_slice(h)))
+
+        w1_bf, w1_w, w1_sc = {}, {}, {}
+
+        def round_w1(a, b):
+            w1_bf[a, b] = held("w1_bf%d%d" % (a, b), [P, KP * PACK], BF16)
+            dealt = w1_bf[a, b][:].rearrange("p (t m j) -> p m j t", t=PACK, j=PACK)
+            for n in range(2):
+                nc.scalar.copy(
+                    out=dealt[:, n * P // 2 : (n + 1) * P // 2],
+                    in_=w1_raw[a, b, n][:].rearrange("p j (m t) -> p m j t", t=PACK),
+                )
+
+        def quantize(name, src, width=512):
+            words = held(name + "_w", [P, width], U32)
+            scales = held(name + "_sc", [P, width], U8)
+            nc.vector.quantize_mx(out=words[:].bitcast(FP8X4), scales=scales[:], in_=src[:])
+            return words, scales
+
+        def quantize_w1(a, b):
+            w1_w[a, b], w1_sc[a, b] = quantize("w1q%d%d" % (a, b), w1_bf[a, b])
+
+        gather_new(0)
+        round_w1(0, 0)
+        gather_new(1)
+        quantize_w1(0, 0)
+        gather_known(0, 0)
+        gather_known_scales(0)
+
+        make_identity(nc, ident[:])
+        bar_t = bank("sine")
+        nc.tensor.transpose(bar_t[:, 0:P], bar_rows[:], ident[:])
+        neg_bar = held("neg_bar", [P, S2 // P], F32)
+        nc.scalar.mul(neg_bar[:], bar_t[:, 0 : S2 // P], -1.0)
+
+        h2_q = []
+
+        def plain_reading(b):
+            h2_bf = held("h2_bf%d" % b, [P, S * PACK], BF16)
+            for jq in range(S // P):
+                acc = bank("plain")
+                js = slice(P * jq, P * (jq + 1))
+                for t in range(PACK):
+                    c0 = KP * b + P * t
+                    for a in range(PASSES):
+                        nc.tensor.matmul_mx(
+                            out=acc[:, P * t : P * (t + 1)],
+                            lhsT=w4_w[a][:, 2 * c0 : 2 * (c0 + P)].bitcast(FP4X4),
+                            lhsT_scale=w4_sc[:, K * a + c0 : K * a + c0 + P],
+                            rhs=v_w[a][:, js].bitcast(FP8X4),
+                            rhs_scale=(v_sc, v_sc1)[a][:, js],
+                            start=(a == 0),
+                            stop=(a == PASSES - 1),
+                        )
+                nc.vector.tensor_tensor(
+                    out=h2_bf[:, KP * jq : KP * (jq + 1)].rearrange("p (j t) -> p j t", t=PACK),
+                    in0=acc[:].rearrange("p (t j) -> p j t", t=PACK),
+                    in1=g2[:, b : b + 1, :].to_broadcast([P, P, PACK]),
+                    op=ALU.mult,
+                )
+            h2_q.append(quantize("h2q%d" % b, h2_bf))
+
+        h1_q, sines = {}, {}
+
+        def sine_reading(b, jh):
+            js = slice(JH * jh, JH * (jh + 1))
+            name = "%d%d" % (b, jh)
+            s = held("s" + name, [P, PACK, JH], F32)
+            sq = held("sq" + name, [P, PACK, JH], F32)
+            sines[b, jh] = s, sq
+            for tp in range(PACK // 2):
+                acc = bank("sine")
+                ts = slice(2 * tp, 2 * tp + 2)
+                for t in range(2 * tp, 2 * tp + 2):
+                    cs = slice(P * t, P * (t + 1))
+                    for a in range(PASSES):
+                        nc.tensor.matmul_mx(
+                            out=acc[:, JH * (t % 2) : JH * (t % 2 + 1)],
+                            lhsT=w1_w[a, b][:, cs].bitcast(FP8X4),
+                            lhsT_scale=w1_sc[a, b][:, cs],
+                            rhs=v_w[a][:, js].bitcast(FP8X4),
+                            rhs_scale=v_sc[ROWS * a : P, js],
+                            start=(a == 0),
+                            stop=(a == PASSES - 1),
+                        )
+                s_pair = s[:, ts, :].rearrange("p t j -> p (t j)")
+                nc.scalar.activation(out=s_pair, in_=acc[:], func=ACT.Sin, scale=-1.0 / 3.0)
+                nc.scalar.activation(
+                    out=sq[:, ts, :].rearrange("p t j -> p (t j)"), in_=s_pair, func=ACT.Square, scale=2.0
+                )
+
+        def triple_angle(b, jh):
+            name = "%d%d" % (b, jh)
+            s, sq = sines[b, jh]
+            u = held("u" + name, [P, PACK, JH], F32)
+            h1_bf = held("h1_bf" + name, [P, JH * PACK], BF16)
+            for t in range(PACK):
+                nc.vector.tensor_scalar(
+                    out=u[:, t, :], in0=sq[:, t, :], scalar1=3.0, scalar2=g1[:, b, t : t + 1],
+                    op0=ALU.subtract, op1=ALU.mult,
+                )
+            nc.vector.tensor_tensor(
+                out=h1_bf[:].rearrange("p (c i t) -> p c t i", i=4, t=PACK),
+                in0=s[:].rearrange("p t (c i) -> p c t i", i=4),
+                in1=u[:].rearrange("p t (c i) -> p c t i", i=4),
+                op=ALU.mult,
+            )
+            h1_q[b, jh] = quantize("h1q" + name, h1_bf, JH)
+
+        def score(acc, c, words, scales):
+            h, cs = c // 4, slice(P * (c % 4), P * (c % 4 + 1))
+            for a in range(PASSES):
+                nc.tensor.matmul_mx(
+                    out=acc,
+                    lhsT=v2_w[a, h][:, cs].bitcast(FP8X4),
+                    lhsT_scale=v2_sc[h][ROWS * a : P, cs],
+                    rhs=words[a][:].bitcast(FP8X4),
+                    rhs_scale=scales[a][:],
+                    start=(a == 0),
+                    stop=(a == PASSES - 1),
+                )
+
+        e2 = []
+
+        def plain_scores(cp):
+            e2.append(held("e2_%d" % cp, [P, 2, S], F32))
+            for ci in range(2):
+                acc = bank("plain")
+                score(acc[:], 2 * cp + ci, [q[0] for q in h2_q], [q[1] for q in h2_q])
+                nc.scalar.copy(out=e2[cp][:, ci, :], in_=acc[:])
+
+        def finish(cp, jh):
+            js = slice(JH * jh, JH * (jh + 1))
+            acc = bank(("sine", "plain")[jh])
+            for ci in range(2):
+                score(
+                    acc[:, JH * ci : JH * (ci + 1)], 2 * cp + ci,
+                    [h1_q[b, jh][0] for b in range(PASSES)], [h1_q[b, jh][1] for b in range(PASSES)],
+                )
+            top = ring.tile([P, 2, JH], F32, name="top")
+            nc.vector.tensor_tensor(
+                out=top[:], in0=acc[:].rearrange("p (c j) -> p c j", c=2), in1=e2[cp][:, :, js], op=ALU.max
+            )
+            res = ring.tile([P, 2, JH], F32, name="res")
+            for ci in range(2):
+                c = 2 * cp + ci
+                nc.scalar.activation(out=res[:, ci, :], in_=top[:, ci, :], func=ACT.Tanh, bias=neg_bar[:, c : c + 1])
+            nc.sync.dma_start(
+                out=out[2 * P * cp : 2 * P * (cp + 1), js].rearrange("(c p) j -> p c j", p=P), in_=res[:]
+            )
+
+        round_w1(1, 0)
+        quantize_w1(1, 0)
+        round_w1(0, 1)
+        quantize_w1(0, 1)
+        round_w1(1, 1)
+        quantize_w1(1, 1)
+        plain_reading(0)
+        plain_reading(1)
+        gather_known_scales(1)
+        gather_known(1, 0)
+        gather_known(0, 1)
+        gather_known(1, 1)
+        for jh in range(2):
+            for b in range(PASSES):
+                sine_reading(b, jh)
+        for cp in range(4):
+            plain_scores(cp)
+        for jh in range(2):
+            for b in range(PASSES):
+                triple_angle(b, jh)
+        for jh in range(2):
+            for cp in range(4):
+                finish(cp, jh)

@@ -47,31 +47,26 @@ def tile_list_fluke_sighting_scores_kernel(
         known_list = lists.tile([P, S2 // 16], U16, name="known_list")
 
         tab_sc = held("tab_sc", [P, T], U8)
-        tab_sc1 = held("tab_sc1", [P, T], U8)
+        tab_sc_rows = held("tab_sc_rows", [P, T], U8)
         w4_sc_raw = held("w4_sc_raw", [P, PASSES * K], U8)
         nc.vector.memset(tab_sc[:].bitcast(I32), 0)
-        nc.vector.memset(tab_sc1[:].bitcast(I32), 0)
         bar_rows = held("bar_rows", [P, P], F32)
-        nc.gpsimd.memset(bar_rows[:], 0.0)
+        warm = held("warm", [P, 2], F32)
+        nc.gpsimd.memset(warm[:, 0:1], 0.0)
+        nc.scalar.activation(out=warm[:, 1:2], in_=warm[:, 0:1], func=ACT.Silu)
         nc.gpsimd.memset(w4_sc_raw[:].bitcast(I32), 0)
+        nc.gpsimd.memset(bar_rows[:], 0.0)
 
-        def load_scales(queue, dst, src):
-            for q in range(QUADS):
-                queue.dma_start(
-                    out=dst[32 * q : 32 * q + PASSES * ROWS, :].bitcast(I32),
-                    in_=src[:, ROWS * q : ROWS * (q + 1), :].bitcast(I32),
-                )
-
-        def load_scales1():
+        def load_tab_scales():
             for q in range(QUADS):
                 nc.sync.dma_start(
-                    out=tab_sc1[32 * q : 32 * q + ROWS, :].bitcast(I32),
-                    in_=tab_scales[1, ROWS * q : ROWS * (q + 1), :].bitcast(I32),
+                    out=tab_sc_rows[32 * q : 32 * q + PASSES * ROWS, :].bitcast(I32),
+                    in_=tab_scales[:, ROWS * q : ROWS * (q + 1), :].bitcast(I32),
                 )
 
         def load_w4_scales():
             for q in range(QUADS):
-                nc.gpsimd.dma_start(
+                nc.sync.dma_start(
                     out=w4_sc_raw[32 * q : 32 * q + ROWS, :].bitcast(I32).rearrange("r (a n) -> r a n", a=PASSES),
                     in_=w4_scales[:, ROWS * q : ROWS * (q + 1), :].bitcast(I32).rearrange("a r n -> r a n"),
                 )
@@ -99,29 +94,33 @@ def tile_list_fluke_sighting_scores_kernel(
         g2 = held("g2", [P, PASSES, PACK], F32)
         ident = held("ident", [P, P], F32)
 
+        load_tab_scales()
         nc.sync.dma_start(new_list[:], offs)
         nc.sync.dma_start(known_list[:], offs2)
-        nc.sync.dma_start(out=g2[:], in_=gain2.rearrange("(b p t) -> p b t", p=P, t=PACK))
-        nc.sync.dma_start(out=g1[:], in_=gain1.rearrange("(b p t) -> p b t", p=P, t=PACK))
-        load_words(0)
         nc.sync.dma_start(
             out=w4_raw[:].bitcast(I32).rearrange("p (a n) -> p a n", a=PASSES),
             in_=w4_words.bitcast(I32).rearrange("a p n -> p a n"),
         )
         load_w1(0, 0)
-        load_scales(nc.sync, tab_sc, tab_scales)
-        load_words(1)
+        load_words(0)
         nc.sync.dma_start(out=bar_rows[0 : S2 // P, :], in_=bar.rearrange("(c p) -> c p", p=P))
-        load_scales1()
         load_w4_scales()
+        load_words(1)
         load_w1(1, 0)
+        nc.sync.dma_start(out=g2[:], in_=gain2.rearrange("(b p t) -> p b t", p=P, t=PACK))
+        nc.sync.dma_start(out=g1[:], in_=gain1.rearrange("(b p t) -> p b t", p=P, t=PACK))
         load_w1(0, 1)
         load_w1(1, 1)
+
+        for q in range(QUADS):
+            rows = slice(32 * q, 32 * q + PASSES * ROWS)
+            nc.vector.tensor_copy(out=tab_sc[rows, :].bitcast(I32), in_=tab_sc_rows[rows, :].bitcast(I32))
 
         v_sc = held("v_sc", [P, S], U8)
         v_sc1 = held("v_sc1", [P, S], U8)
         nc.vector.tensor_copy(v_sc[:], tab_sc[:].indirect(new_list[:]))
-        nc.vector.tensor_copy(v_sc1[:], tab_sc1[:].indirect(new_list[:]))
+        nc.vector.memset(v_sc1[:].bitcast(I32), 0)
+        nc.gpsimd.dma_start(out=v_sc1[0 : P - ROWS, :].bitcast(I32), in_=v_sc[ROWS:P, :].bitcast(I32))
 
         def known_slice(h):
             return known_list[:, h * HALF // 16 : (h + 1) * HALF // 16]
@@ -129,7 +128,7 @@ def tile_list_fluke_sighting_scores_kernel(
         v2_sc = {}
 
         def gather_known_scales(h):
-            v2_sc[h] = held("v2_sc%d" % h, [P, HALF], U8, tag=("", "w1_bf00")[h])
+            v2_sc[h] = held("v2_sc%d" % h, [P, HALF], U8)
             nc.vector.tensor_copy(v2_sc[h][:], tab_sc[:].indirect(known_slice(h)))
 
         w4_sc = held("w4_sc", [P, PASSES * K], U8)
@@ -152,8 +151,7 @@ def tile_list_fluke_sighting_scores_kernel(
             nc.vector.tensor_copy(v_w[a][:], tab_w[a][:].indirect(new_list[:]))
 
         def gather_known(a, h):
-            tag = {(1, 0): "w1_bf10", (1, 1): "w1_bf01"}.get((a, h), "")
-            v2_w[a, h] = held("v2_w%d%d" % (a, h), [P, HALF], U32, tag=tag)
+            v2_w[a, h] = held("v2_w%d%d" % (a, h), [P, HALF], U32, tag=(("w1_bf10", "w1_bf11")[h], "")[a])
             nc.vector.tensor_copy(v2_w[a, h][:], tab_w[a][:].indirect(known_slice(h)))
 
         w1_bf, w1_w, w1_sc = {}, {}, {}
@@ -180,14 +178,15 @@ def tile_list_fluke_sighting_scores_kernel(
         round_w1(0, 0)
         gather_new(1)
         quantize_w1(0, 0)
-        gather_known(0, 0)
         gather_known_scales(0)
 
         make_identity(nc, ident[:])
         bar_t = bank("sine")
         nc.tensor.transpose(bar_t[:, 0:P], bar_rows[:], ident[:])
         neg_bar = held("neg_bar", [P, S2 // P], F32)
-        nc.scalar.mul(neg_bar[:], bar_t[:, 0 : S2 // P], -1.0)
+        nc.vector.tensor_scalar(
+            out=neg_bar[:], in0=bar_t[:, 0 : S2 // P], scalar1=-1.0, scalar2=None, op0=ALU.mult
+        )
 
         h2_q = []
 
@@ -221,7 +220,7 @@ def tile_list_fluke_sighting_scores_kernel(
         def sine_reading(b, jh):
             js = slice(JH * jh, JH * (jh + 1))
             name = "%d%d" % (b, jh)
-            s = held("s" + name, [P, PACK, JH], F32)
+            s = held("s" + name, [P, PACK, JH], F32, tag={"00": "w1_raw111"}.get(name, ""))
             sq = held("sq" + name, [P, PACK, JH], F32)
             sines[b, jh] = s, sq
             for tp in range(PACK // 2):
@@ -315,15 +314,16 @@ def tile_list_fluke_sighting_scores_kernel(
         plain_reading(1)
         gather_known_scales(1)
         gather_known(1, 0)
+        gather_known(0, 0)
         gather_known(0, 1)
         gather_known(1, 1)
-        for jh in range(2):
-            for b in range(PASSES):
+        for b in range(PASSES):
+            for jh in range(2):
                 sine_reading(b, jh)
         for cp in range(4):
             plain_scores(cp)
-        for jh in range(2):
-            for b in range(PASSES):
+        for b in range(PASSES):
+            for jh in range(2):
                 triple_angle(b, jh)
         for jh in range(2):
             for cp in range(4):

@@ -22,9 +22,13 @@ PACK = 4
 KP = P * PACK
 PASSES = K // KP
 QUADS = 4
-ROWS = 4
-HALF = 512
+SC_ROWS = 4
+BANK = 512
+LIST_COL = 16
+KNOWN_HALF = S2 // 2
+TILES_PER_HALF = KNOWN_HALF // P
 JH = S // 2
+LINE = 16
 
 
 def tile_list_fluke_sighting_scores_kernel(
@@ -34,51 +38,43 @@ def tile_list_fluke_sighting_scores_kernel(
     with ExitStack() as ctx:
         lists = ctx.enter_context(tc.tile_pool(name="lists", bufs=1))
         keep = ctx.enter_context(tc.tile_pool(name="keep", bufs=1))
-        ring = ctx.enter_context(tc.tile_pool(name="ring", bufs=8))
+        results = ctx.enter_context(tc.tile_pool(name="results", bufs=8))
         psum = ctx.enter_context(tc.psum_pool(name="psum", bufs=4))
 
-        def held(name, shape, dtype, tag=""):
-            return keep.tile(shape, dtype, name=name, tag=tag or name, align_bytes=64)
+        def held(name, shape, dtype, over=""):
+            return keep.tile(shape, dtype, name=name, tag=over or name, align_bytes=64)
 
         def bank(tag):
-            return psum.tile([P, 512], F32, name=tag)
+            return psum.tile([P, BANK], F32, name=tag)
 
-        new_list = lists.tile([P, S // 16], U16, name="new_list")
-        known_list = lists.tile([P, S2 // 16], U16, name="known_list")
-
-        tab_sc = held("tab_sc", [P, T], U8)
+        new_list = lists.tile([P, S // LIST_COL], U16, name="new_list")
+        known_list = lists.tile([P, S2 // LIST_COL], U16, name="known_list")
         tab_sc_rows = held("tab_sc_rows", [P, T], U8)
+        tab_sc = held("tab_sc", [P, T], U8)
+        tab_w = [held("tab_w%d" % a, [P, T], U32) for a in range(PASSES)]
+        w4_raw = held("w4_raw", [P, PASSES * 2 * K], U8)
         w4_sc_raw = held("w4_sc_raw", [P, PASSES * K], U8)
-        nc.vector.memset(tab_sc[:].bitcast(I32), 0)
+        g1 = held("g1", [P, PASSES, PACK], F32)
+        g2 = held("g2", [P, PASSES, PACK], F32)
         bar_rows = held("bar_rows", [P, P], F32)
+        ident = held("ident", [P, P], F32)
+        new_sc = held("new_sc", [P, S], U8)
+        new_sc1 = held("new_sc1", [P, S], U8)
+        w1_raw = {}
+
+        nc.vector.memset(tab_sc[:].bitcast(I32), 0)
+        nc.vector.memset(new_sc1[:].bitcast(I32), 0)
         warm = held("warm", [P, 2], F32)
         nc.gpsimd.memset(warm[:, 0:1], 0.0)
         nc.scalar.activation(out=warm[:, 1:2], in_=warm[:, 0:1], func=ACT.Silu)
         nc.gpsimd.memset(w4_sc_raw[:].bitcast(I32), 0)
         nc.gpsimd.memset(bar_rows[:], 0.0)
-
-        def load_tab_scales():
-            for q in range(QUADS):
-                nc.sync.dma_start(
-                    out=tab_sc_rows[32 * q : 32 * q + PASSES * ROWS, :].bitcast(I32),
-                    in_=tab_scales[:, ROWS * q : ROWS * (q + 1), :].bitcast(I32),
-                )
-
-        def load_w4_scales():
-            for q in range(QUADS):
-                nc.sync.dma_start(
-                    out=w4_sc_raw[32 * q : 32 * q + ROWS, :].bitcast(I32).rearrange("r (a n) -> r a n", a=PASSES),
-                    in_=w4_scales[:, ROWS * q : ROWS * (q + 1), :].bitcast(I32).rearrange("a r n -> r a n"),
-                )
-
-        tab_w = [held("tab_w%d" % a, [P, T], U32) for a in range(PASSES)]
-        w4_raw = held("w4_raw", [P, PASSES * 2 * K], U8)
-        w1_raw = {}
+        make_identity(nc, ident[:])
 
         def load_words(a):
             nc.sync.dma_start(
                 out=tab_w[a][:].bitcast(I32),
-                in_=tab_words[a].rearrange("p n t -> p (n t)").bitcast(I32),
+                in_=tab_words[a].rearrange("p n i -> p (n i)").bitcast(I32),
             )
 
         def load_w1(a, b):
@@ -87,125 +83,99 @@ def tile_list_fluke_sighting_scores_kernel(
                 c0 = KP * b + n * KP // 2
                 nc.sync.dma_start(
                     out=w1_raw[a, b, n][:],
-                    in_=w1[KP * a : KP * (a + 1), c0 : c0 + KP // 2].rearrange("(p j) c -> p j c", j=PACK),
+                    in_=w1[KP * a : KP * (a + 1), c0 : c0 + KP // 2].rearrange("(p i) c -> p i c", i=PACK),
                 )
 
-        g1 = held("g1", [P, PASSES, PACK], F32)
-        g2 = held("g2", [P, PASSES, PACK], F32)
-        ident = held("ident", [P, P], F32)
+        def load_gain(dst, src):
+            nc.sync.dma_start(out=dst[:], in_=src.rearrange("(b p t) -> p b t", p=P, t=PACK))
 
-        load_tab_scales()
+        for q in range(QUADS):
+            nc.sync.dma_start(
+                out=tab_sc_rows[32 * q : 32 * q + PASSES * SC_ROWS, :].bitcast(I32),
+                in_=tab_scales[:, SC_ROWS * q : SC_ROWS * (q + 1), :].bitcast(I32),
+            )
         nc.sync.dma_start(new_list[:], offs)
         nc.sync.dma_start(known_list[:], offs2)
         nc.sync.dma_start(
             out=w4_raw[:].bitcast(I32).rearrange("p (a n) -> p a n", a=PASSES),
             in_=w4_words.bitcast(I32).rearrange("a p n -> p a n"),
         )
-        load_w1(0, 0)
         load_words(0)
-        nc.sync.dma_start(out=bar_rows[0 : S2 // P, :], in_=bar.rearrange("(c p) -> c p", p=P))
-        load_w4_scales()
-        load_words(1)
+        load_w1(0, 0)
+        for q in range(QUADS):
+            nc.sync.dma_start(
+                out=w4_sc_raw[32 * q : 32 * q + SC_ROWS, :].bitcast(I32).rearrange("r (a n) -> r a n", a=PASSES),
+                in_=w4_scales[:, SC_ROWS * q : SC_ROWS * (q + 1), :].bitcast(I32).rearrange("a r n -> r a n"),
+            )
         load_w1(1, 0)
-        nc.sync.dma_start(out=g2[:], in_=gain2.rearrange("(b p t) -> p b t", p=P, t=PACK))
-        nc.sync.dma_start(out=g1[:], in_=gain1.rearrange("(b p t) -> p b t", p=P, t=PACK))
-        load_w1(0, 1)
-        load_w1(1, 1)
 
         for q in range(QUADS):
-            rows = slice(32 * q, 32 * q + PASSES * ROWS)
+            rows = slice(32 * q, 32 * q + PASSES * SC_ROWS)
             nc.vector.tensor_copy(out=tab_sc[rows, :].bitcast(I32), in_=tab_sc_rows[rows, :].bitcast(I32))
-
-        v_sc = held("v_sc", [P, S], U8)
-        v_sc1 = held("v_sc1", [P, S], U8)
-        nc.vector.tensor_copy(v_sc[:], tab_sc[:].indirect(new_list[:]))
-        nc.vector.memset(v_sc1[:].bitcast(I32), 0)
-        nc.gpsimd.dma_start(out=v_sc1[0 : P - ROWS, :].bitcast(I32), in_=v_sc[ROWS:P, :].bitcast(I32))
-
-        def known_slice(h):
-            return known_list[:, h * HALF // 16 : (h + 1) * HALF // 16]
-
-        v2_sc = {}
-
-        def gather_known_scales(h):
-            v2_sc[h] = held("v2_sc%d" % h, [P, HALF], U8)
-            nc.vector.tensor_copy(v2_sc[h][:], tab_sc[:].indirect(known_slice(h)))
-
-        w4_sc = held("w4_sc", [P, PASSES * K], U8)
-        nc.vector.tensor_copy(
-            out=w4_sc[:].rearrange("p (g t o i) -> p g o t i", g=PASSES * PASSES, t=PACK, i=16),
-            in_=w4_sc_raw[:].rearrange("p (g o i t) -> p g o t i", g=PASSES * PASSES, t=PACK, i=16),
+        nc.vector.tensor_copy(new_sc[:], tab_sc[:].indirect(new_list[:]))
+        nc.sync.dma_start(
+            out=new_sc1[0 : P - SC_ROWS, :].bitcast(I32), in_=new_sc[SC_ROWS:P, :].bitcast(I32)
         )
 
-        w4_w = [held("w4_w%d" % a, [P, 2 * K], U8) for a in range(PASSES)]
-        for a in range(PASSES):
-            nc.scalar.copy(
-                out=w4_w[a][:].bitcast(U16).rearrange("p (b t o i) -> p b o t i", b=PASSES, t=PACK, i=8),
-                in_=w4_raw[:, 2 * K * a : 2 * K * (a + 1)].bitcast(U16).rearrange("p (b o i t) -> p b o t i", b=PASSES, t=PACK, i=8),
-            )
+        load_words(1)
+        nc.sync.dma_start(out=bar_rows[0 : S2 // P, :], in_=bar.rearrange("(c p) -> c p", p=P))
+        load_w1(0, 1)
+        load_gain(g2, gain2)
+        load_w1(1, 1)
+        load_gain(g1, gain1)
 
-        v_w = [held("v_w%d" % a, [P, S], U32) for a in range(PASSES)]
-        v2_w = {}
+        new_w, known_w, known_sc = {}, {}, {}
+        w1_bf, w1_q, h2_q, h1_q, sines, e2 = {}, {}, {}, {}, {}, {}
 
-        def gather_new(a):
-            nc.vector.tensor_copy(v_w[a][:], tab_w[a][:].indirect(new_list[:]))
+        def known_slice(h):
+            return known_list[:, h * KNOWN_HALF // LIST_COL : (h + 1) * KNOWN_HALF // LIST_COL]
 
-        def gather_known(a, h):
-            v2_w[a, h] = held("v2_w%d%d" % (a, h), [P, HALF], U32, tag=(("w1_bf10", "w1_bf11")[h], "")[a])
-            nc.vector.tensor_copy(v2_w[a, h][:], tab_w[a][:].indirect(known_slice(h)))
+        def gather_new_words(a):
+            new_w[a] = held("new_w%d" % a, [P, S], U32)
+            nc.vector.tensor_copy(new_w[a][:], tab_w[a][:].indirect(new_list[:]))
 
-        w1_bf, w1_w, w1_sc = {}, {}, {}
+        def gather_known_words(a, h, over=""):
+            known_w[a, h] = held("known_w%d%d" % (a, h), [P, KNOWN_HALF], U32, over)
+            nc.vector.tensor_copy(known_w[a, h][:], tab_w[a][:].indirect(known_slice(h)))
 
-        def round_w1(a, b):
-            w1_bf[a, b] = held("w1_bf%d%d" % (a, b), [P, KP * PACK], BF16)
-            dealt = w1_bf[a, b][:].rearrange("p (t m j) -> p m j t", t=PACK, j=PACK)
-            for n in range(2):
-                nc.scalar.copy(
-                    out=dealt[:, n * P // 2 : (n + 1) * P // 2],
-                    in_=w1_raw[a, b, n][:].rearrange("p j (m t) -> p m j t", t=PACK),
-                )
+        def gather_known_scales(h):
+            known_sc[h] = held("known_sc%d" % h, [P, KNOWN_HALF], U8)
+            nc.vector.tensor_copy(known_sc[h][:], tab_sc[:].indirect(known_slice(h)))
 
-        def quantize(name, src, width=512):
+        def quantize(name, src, width):
             words = held(name + "_w", [P, width], U32)
             scales = held(name + "_sc", [P, width], U8)
             nc.vector.quantize_mx(out=words[:].bitcast(FP8X4), scales=scales[:], in_=src[:])
             return words, scales
 
+        def round_w1(a, b):
+            w1_bf[a, b] = held("w1_bf%d%d" % (a, b), [P, KP * PACK], BF16)
+            dealt = w1_bf[a, b][:].rearrange("p (t m i) -> p m i t", t=PACK, i=PACK)
+            for n in range(2):
+                nc.scalar.copy(
+                    out=dealt[:, n * P // 2 : (n + 1) * P // 2],
+                    in_=w1_raw[a, b, n][:].rearrange("p i (m t) -> p m i t", t=PACK),
+                )
+
         def quantize_w1(a, b):
-            w1_w[a, b], w1_sc[a, b] = quantize("w1q%d%d" % (a, b), w1_bf[a, b])
-
-        gather_new(0)
-        round_w1(0, 0)
-        gather_new(1)
-        quantize_w1(0, 0)
-        gather_known_scales(0)
-
-        make_identity(nc, ident[:])
-        bar_t = bank("sine")
-        nc.tensor.transpose(bar_t[:, 0:P], bar_rows[:], ident[:])
-        neg_bar = held("neg_bar", [P, S2 // P], F32)
-        nc.vector.tensor_scalar(
-            out=neg_bar[:], in0=bar_t[:, 0 : S2 // P], scalar1=-1.0, scalar2=None, op0=ALU.mult
-        )
-
-        h2_q = []
+            w1_q[a, b] = quantize("w1q%d%d" % (a, b), w1_bf[a, b], KP)
 
         def plain_reading(b):
             h2_bf = held("h2_bf%d" % b, [P, S * PACK], BF16)
             for jq in range(S // P):
-                acc = bank("plain")
+                acc = bank("w4")
                 js = slice(P * jq, P * (jq + 1))
-                for t in range(PACK):
-                    c0 = KP * b + P * t
-                    for a in range(PASSES):
+                for a in range(PASSES):
+                    for t in range(PACK):
+                        c0 = KP * b + P * t
                         nc.tensor.matmul_mx(
                             out=acc[:, P * t : P * (t + 1)],
                             lhsT=w4_w[a][:, 2 * c0 : 2 * (c0 + P)].bitcast(FP4X4),
                             lhsT_scale=w4_sc[:, K * a + c0 : K * a + c0 + P],
-                            rhs=v_w[a][:, js].bitcast(FP8X4),
-                            rhs_scale=(v_sc, v_sc1)[a][:, js],
-                            start=(a == 0),
-                            stop=(a == PASSES - 1),
+                            rhs=new_w[a][:, js].bitcast(FP8X4),
+                            rhs_scale=(new_sc, new_sc1)[a][:, js],
+                            start=(a, t) == (0, 0),
+                            stop=(a, t) == (PASSES - 1, PACK - 1),
                         )
                 nc.vector.tensor_tensor(
                     out=h2_bf[:, KP * jq : KP * (jq + 1)].rearrange("p (j t) -> p j t", t=PACK),
@@ -213,90 +183,83 @@ def tile_list_fluke_sighting_scores_kernel(
                     in1=g2[:, b : b + 1, :].to_broadcast([P, P, PACK]),
                     op=ALU.mult,
                 )
-            h2_q.append(quantize("h2q%d" % b, h2_bf))
+            h2_q[b] = quantize("h2q%d" % b, h2_bf, S)
 
-        h1_q, sines = {}, {}
+        def third_angle(b, jh):
+            js = slice(JH * jh, JH * (jh + 1))
+            s = held("s%d%d" % (b, jh), [P, PACK * JH], F32)
+            sq = held("sq%d%d" % (b, jh), [P, PACK * JH], F32)
+            sines[b, jh] = s, sq
+            for pair in range(PACK // 2):
+                acc = bank("w1")
+                for a in range(PASSES):
+                    words, scales = w1_q[a, b]
+                    for ti in range(2):
+                        cs = slice(P * (2 * pair + ti), P * (2 * pair + ti + 1))
+                        nc.tensor.matmul_mx(
+                            out=acc[:, JH * ti : JH * (ti + 1)],
+                            lhsT=words[:, cs].bitcast(FP8X4),
+                            lhsT_scale=scales[:, cs],
+                            rhs=new_w[a][:, js].bitcast(FP8X4),
+                            rhs_scale=new_sc[SC_ROWS * a : P, js],
+                            start=(a, ti) == (0, 0),
+                            stop=(a, ti) == (PASSES - 1, 1),
+                        )
+                cols = slice(BANK * pair, BANK * (pair + 1))
+                nc.scalar.activation(out=s[:, cols], in_=acc[:], func=ACT.Sin, scale=-1.0 / 3.0)
+                nc.scalar.activation(out=sq[:, cols], in_=s[:, cols], func=ACT.Square, scale=2.0)
 
         def sine_reading(b, jh):
-            js = slice(JH * jh, JH * (jh + 1))
-            name = "%d%d" % (b, jh)
-            s = held("s" + name, [P, PACK, JH], F32, tag={"00": "w1_raw111"}.get(name, ""))
-            sq = held("sq" + name, [P, PACK, JH], F32)
-            sines[b, jh] = s, sq
-            for tp in range(PACK // 2):
-                acc = bank("sine")
-                ts = slice(2 * tp, 2 * tp + 2)
-                for t in range(2 * tp, 2 * tp + 2):
-                    cs = slice(P * t, P * (t + 1))
-                    for a in range(PASSES):
-                        nc.tensor.matmul_mx(
-                            out=acc[:, JH * (t % 2) : JH * (t % 2 + 1)],
-                            lhsT=w1_w[a, b][:, cs].bitcast(FP8X4),
-                            lhsT_scale=w1_sc[a, b][:, cs],
-                            rhs=v_w[a][:, js].bitcast(FP8X4),
-                            rhs_scale=v_sc[ROWS * a : P, js],
-                            start=(a == 0),
-                            stop=(a == PASSES - 1),
-                        )
-                s_pair = s[:, ts, :].rearrange("p t j -> p (t j)")
-                nc.scalar.activation(out=s_pair, in_=acc[:], func=ACT.Sin, scale=-1.0 / 3.0)
-                nc.scalar.activation(
-                    out=sq[:, ts, :].rearrange("p t j -> p (t j)"), in_=s_pair, func=ACT.Square, scale=2.0
-                )
-
-        def triple_angle(b, jh):
-            name = "%d%d" % (b, jh)
             s, sq = sines[b, jh]
-            u = held("u" + name, [P, PACK, JH], F32)
-            h1_bf = held("h1_bf" + name, [P, JH * PACK], BF16)
+            u = held("u%d%d" % (b, jh), [P, PACK * JH], F32)
             for t in range(PACK):
+                cols = slice(JH * t, JH * (t + 1))
                 nc.vector.tensor_scalar(
-                    out=u[:, t, :], in0=sq[:, t, :], scalar1=3.0, scalar2=g1[:, b, t : t + 1],
+                    out=u[:, cols], in0=sq[:, cols], scalar1=3.0, scalar2=g1[:, b, t : t + 1],
                     op0=ALU.subtract, op1=ALU.mult,
                 )
+            h1_bf = held("h1_bf%d%d" % (b, jh), [P, JH * PACK], BF16)
             nc.vector.tensor_tensor(
-                out=h1_bf[:].rearrange("p (c i t) -> p c t i", i=4, t=PACK),
-                in0=s[:].rearrange("p t (c i) -> p c t i", i=4),
-                in1=u[:].rearrange("p t (c i) -> p c t i", i=4),
+                out=h1_bf[:].rearrange("p (c n t) -> p c t n", n=LINE // 4, t=PACK),
+                in0=s[:].rearrange("p (t c n) -> p c t n", t=PACK, n=LINE // 4),
+                in1=u[:].rearrange("p (t c n) -> p c t n", t=PACK, n=LINE // 4),
                 op=ALU.mult,
             )
-            h1_q[b, jh] = quantize("h1q" + name, h1_bf, JH)
+            h1_q[b, jh] = quantize("h1q%d%d" % (b, jh), h1_bf, JH)
 
-        def score(acc, c, words, scales):
-            h, cs = c // 4, slice(P * (c % 4), P * (c % 4 + 1))
+        def score(acc, tiles, h_q):
+            width = BANK // len(tiles)
             for a in range(PASSES):
-                nc.tensor.matmul_mx(
-                    out=acc,
-                    lhsT=v2_w[a, h][:, cs].bitcast(FP8X4),
-                    lhsT_scale=v2_sc[h][ROWS * a : P, cs],
-                    rhs=words[a][:].bitcast(FP8X4),
-                    rhs_scale=scales[a][:],
-                    start=(a == 0),
-                    stop=(a == PASSES - 1),
-                )
-
-        e2 = []
+                words, scales = h_q[a]
+                for ci, c in enumerate(tiles):
+                    h, ch = divmod(c, TILES_PER_HALF)
+                    cs = slice(P * ch, P * (ch + 1))
+                    nc.tensor.matmul_mx(
+                        out=acc[:, width * ci : width * (ci + 1)],
+                        lhsT=known_w[a, h][:, cs].bitcast(FP8X4),
+                        lhsT_scale=known_sc[h][SC_ROWS * a : P, cs],
+                        rhs=words[:].bitcast(FP8X4),
+                        rhs_scale=scales[:],
+                        start=(a, ci) == (0, 0),
+                        stop=(a, ci) == (PASSES - 1, len(tiles) - 1),
+                    )
 
         def plain_scores(cp):
-            e2.append(held("e2_%d" % cp, [P, 2, S], F32))
+            e2[cp] = held("e2_%d" % cp, [P, 2, S], F32)
             for ci in range(2):
-                acc = bank("plain")
-                score(acc[:], 2 * cp + ci, [q[0] for q in h2_q], [q[1] for q in h2_q])
+                acc = bank("w4")
+                score(acc, [2 * cp + ci], h2_q)
                 nc.scalar.copy(out=e2[cp][:, ci, :], in_=acc[:])
 
         def finish(cp, jh):
             js = slice(JH * jh, JH * (jh + 1))
-            acc = bank(("sine", "plain")[jh])
-            for ci in range(2):
-                score(
-                    acc[:, JH * ci : JH * (ci + 1)], 2 * cp + ci,
-                    [h1_q[b, jh][0] for b in range(PASSES)], [h1_q[b, jh][1] for b in range(PASSES)],
-                )
-            top = ring.tile([P, 2, JH], F32, name="top")
+            acc = bank(("w1", "w4")[jh])
+            score(acc, [2 * cp, 2 * cp + 1], [h1_q[b, jh] for b in range(PASSES)])
+            top = results.tile([P, 2, JH], F32, name="top")
             nc.vector.tensor_tensor(
                 out=top[:], in0=acc[:].rearrange("p (c j) -> p c j", c=2), in1=e2[cp][:, :, js], op=ALU.max
             )
-            res = ring.tile([P, 2, JH], F32, name="res")
+            res = results.tile([P, 2, JH], F32, name="res")
             for ci in range(2):
                 c = 2 * cp + ci
                 nc.scalar.activation(out=res[:, ci, :], in_=top[:, ci, :], func=ACT.Tanh, bias=neg_bar[:, c : c + 1])
@@ -304,27 +267,46 @@ def tile_list_fluke_sighting_scores_kernel(
                 out=out[2 * P * cp : 2 * P * (cp + 1), js].rearrange("(c p) j -> p c j", p=P), in_=res[:]
             )
 
-        round_w1(1, 0)
-        quantize_w1(1, 0)
-        round_w1(0, 1)
-        quantize_w1(0, 1)
-        round_w1(1, 1)
-        quantize_w1(1, 1)
-        plain_reading(0)
-        plain_reading(1)
-        gather_known_scales(1)
-        gather_known(1, 0)
-        gather_known(0, 0)
-        gather_known(0, 1)
-        gather_known(1, 1)
+        w4_w = [held("w4_w%d" % a, [P, 2 * K], U8) for a in range(PASSES)]
+        for a in range(PASSES):
+            nc.scalar.copy(
+                out=w4_w[a][:].bitcast(U16).rearrange("p (b t o n) -> p b o t n", b=PASSES, t=PACK, n=LINE // 2),
+                in_=w4_raw[:, 2 * K * a : 2 * K * (a + 1)]
+                .bitcast(U16)
+                .rearrange("p (b o n t) -> p b o t n", b=PASSES, t=PACK, n=LINE // 2),
+            )
+        w4_sc = held("w4_sc", [P, PASSES * K], U8)
+        nc.vector.tensor_copy(
+            out=w4_sc[:].rearrange("p (g t o n) -> p g o t n", g=PASSES * PASSES, t=PACK, n=LINE),
+            in_=w4_sc_raw[:].rearrange("p (g o n t) -> p g o t n", g=PASSES * PASSES, t=PACK, n=LINE),
+        )
+
+        bar_t = bank("w1")
+        nc.tensor.transpose(bar_t[:, 0:P], bar_rows[:], ident[:])
+        neg_bar = held("neg_bar", [P, S2 // P], F32)
+        nc.vector.tensor_scalar(out=neg_bar[:], in0=bar_t[:, 0 : S2 // P], scalar1=-1.0, scalar2=None, op0=ALU.mult)
+
+        for a in range(PASSES):
+            gather_new_words(a)
+        for b in range(PASSES):
+            for a in range(PASSES):
+                round_w1(a, b)
+                quantize_w1(a, b)
+        for b in range(PASSES):
+            plain_reading(b)
+        for h in range(2):
+            gather_known_scales(h)
+        for a in range(PASSES):
+            for h in range(2):
+                gather_known_words(a, h)
         for b in range(PASSES):
             for jh in range(2):
-                sine_reading(b, jh)
-        for cp in range(4):
+                third_angle(b, jh)
+        for cp in range(S2 // (2 * P)):
             plain_scores(cp)
         for b in range(PASSES):
             for jh in range(2):
-                triple_angle(b, jh)
+                sine_reading(b, jh)
         for jh in range(2):
-            for cp in range(4):
+            for cp in range(S2 // (2 * P)):
                 finish(cp, jh)

from contextlib import ExitStack

import concourse.mybir as mybir
from concourse.masks import make_identity

K, T, S, S2 = 1024, 2048, 512, 1024
FLOPS = 2 * (2 * K * K * S + 2 * K * S2 * S)

F32 = mybir.dt.float32
BF16 = mybir.dt.bfloat16
I32 = mybir.dt.int32
U32 = mybir.dt.uint32
U16 = mybir.dt.uint16
U8 = mybir.dt.uint8
FP8X4 = mybir.dt.float8_e4m3fn_x4
FP4X4 = mybir.dt.float4_e2m1fn_x4
ALU = mybir.AluOpType
ACT = mybir.ActivationFunctionType

P = 128
PACK = 4
KP = P * PACK
PASSES = K // KP
QUADS = 4
SC_ROWS = 4
BANK = 512
LIST_COL = 16
KNOWN_HALF = S2 // 2
TILES_PER_HALF = KNOWN_HALF // P
JH = S // 2
LINE = 16


def tile_list_fluke_sighting_scores_kernel(
    tc, tab_words, tab_scales, offs, offs2, w1, w4_words, w4_scales, gain1, gain2, bar, out
):
    nc = tc.nc
    with ExitStack() as ctx:
        lists = ctx.enter_context(tc.tile_pool(name="lists", bufs=1))
        keep = ctx.enter_context(tc.tile_pool(name="keep", bufs=1))
        results = ctx.enter_context(tc.tile_pool(name="results", bufs=8))
        psum = ctx.enter_context(tc.psum_pool(name="psum", bufs=4))

        def held(name, shape, dtype, over=""):
            return keep.tile(shape, dtype, name=name, tag=over or name, align_bytes=64)

        def bank(tag):
            return psum.tile([P, BANK], F32, name=tag)

        new_list = lists.tile([P, S // LIST_COL], U16, name="new_list")
        known_list = lists.tile([P, S2 // LIST_COL], U16, name="known_list")
        tab_sc_rows = held("tab_sc_rows", [P, T], U8)
        tab_sc = held("tab_sc", [P, T], U8)
        tab_w = [held("tab_w%d" % a, [P, T], U32) for a in range(PASSES)]
        w4_raw = held("w4_raw", [P, PASSES * 2 * K], U8)
        w4_sc_raw = held("w4_sc_raw", [P, PASSES * K], U8)
        g1 = held("g1", [P, PASSES, PACK], F32)
        g2 = held("g2", [P, PASSES, PACK], F32)
        bar_rows = held("bar_rows", [P, P], F32)
        ident = held("ident", [P, P], F32)
        new_sc = held("new_sc", [P, S], U8)
        new_sc1 = held("new_sc1", [P, S], U8)
        w1_raw = {}

        nc.vector.memset(tab_sc[:].bitcast(I32), 0)
        nc.vector.memset(new_sc1[:].bitcast(I32), 0)
        warm = held("warm", [P, 2], F32)
        nc.gpsimd.memset(warm[:, 0:1], 0.0)
        nc.scalar.activation(out=warm[:, 1:2], in_=warm[:, 0:1], func=ACT.Silu)
        nc.gpsimd.memset(w4_sc_raw[:].bitcast(I32), 0)
        nc.gpsimd.memset(bar_rows[:], 0.0)
        make_identity(nc, ident[:])

        def load_words(a):
            nc.sync.dma_start(
                out=tab_w[a][:].bitcast(I32),
                in_=tab_words[a].rearrange("p n i -> p (n i)").bitcast(I32),
            )

        def load_w1(a, b):
            for n in range(2):
                w1_raw[a, b, n] = held("w1_raw%d%d%d" % (a, b, n), [P, PACK, KP // 2], F32)
                c0 = KP * b + n * KP // 2
                nc.sync.dma_start(
                    out=w1_raw[a, b, n][:],
                    in_=w1[KP * a : KP * (a + 1), c0 : c0 + KP // 2].rearrange("(p i) c -> p i c", i=PACK),
                )

        def load_gain(dst, src):
            nc.sync.dma_start(out=dst[:], in_=src.rearrange("(b p t) -> p b t", p=P, t=PACK))

        for q in range(QUADS):
            nc.sync.dma_start(
                out=tab_sc_rows[32 * q : 32 * q + PASSES * SC_ROWS, :].bitcast(I32),
                in_=tab_scales[:, SC_ROWS * q : SC_ROWS * (q + 1), :].bitcast(I32),
            )
        nc.sync.dma_start(new_list[:], offs)
        nc.sync.dma_start(known_list[:], offs2)
        nc.sync.dma_start(
            out=w4_raw[:].bitcast(I32).rearrange("p (a n) -> p a n", a=PASSES),
            in_=w4_words.bitcast(I32).rearrange("a p n -> p a n"),
        )
        load_words(0)
        load_w1(0, 0)
        for q in range(QUADS):
            nc.sync.dma_start(
                out=w4_sc_raw[32 * q : 32 * q + SC_ROWS, :].bitcast(I32).rearrange("r (a n) -> r a n", a=PASSES),
                in_=w4_scales[:, SC_ROWS * q : SC_ROWS * (q + 1), :].bitcast(I32).rearrange("a r n -> r a n"),
            )
        load_w1(1, 0)

        for q in range(QUADS):
            rows = slice(32 * q, 32 * q + PASSES * SC_ROWS)
            nc.vector.tensor_copy(out=tab_sc[rows, :].bitcast(I32), in_=tab_sc_rows[rows, :].bitcast(I32))
        nc.vector.tensor_copy(new_sc[:], tab_sc[:].indirect(new_list[:]))
        nc.sync.dma_start(
            out=new_sc1[0 : P - SC_ROWS, :].bitcast(I32), in_=new_sc[SC_ROWS:P, :].bitcast(I32)
        )

        load_words(1)
        nc.sync.dma_start(out=bar_rows[0 : S2 // P, :], in_=bar.rearrange("(c p) -> c p", p=P))
        load_w1(0, 1)
        load_gain(g2, gain2)
        load_w1(1, 1)
        load_gain(g1, gain1)

        new_w, known_w, known_sc = {}, {}, {}
        w1_bf, w1_q, h2_q, h1_q, sines, e2 = {}, {}, {}, {}, {}, {}

        def known_slice(h):
            return known_list[:, h * KNOWN_HALF // LIST_COL : (h + 1) * KNOWN_HALF // LIST_COL]

        def gather_new_words(a):
            new_w[a] = held("new_w%d" % a, [P, S], U32)
            nc.vector.tensor_copy(new_w[a][:], tab_w[a][:].indirect(new_list[:]))

        def gather_known_words(a, h, over=""):
            known_w[a, h] = held("known_w%d%d" % (a, h), [P, KNOWN_HALF], U32, over)
            nc.vector.tensor_copy(known_w[a, h][:], tab_w[a][:].indirect(known_slice(h)))

        def gather_known_scales(h):
            known_sc[h] = held("known_sc%d" % h, [P, KNOWN_HALF], U8)
            nc.vector.tensor_copy(known_sc[h][:], tab_sc[:].indirect(known_slice(h)))

        def quantize(name, src, width):
            words = held(name + "_w", [P, width], U32)
            scales = held(name + "_sc", [P, width], U8)
            nc.vector.quantize_mx(out=words[:].bitcast(FP8X4), scales=scales[:], in_=src[:])
            return words, scales

        def round_w1(a, b):
            w1_bf[a, b] = held("w1_bf%d%d" % (a, b), [P, KP * PACK], BF16)
            dealt = w1_bf[a, b][:].rearrange("p (t m i) -> p m i t", t=PACK, i=PACK)
            for n in range(2):
                nc.scalar.copy(
                    out=dealt[:, n * P // 2 : (n + 1) * P // 2],
                    in_=w1_raw[a, b, n][:].rearrange("p i (m t) -> p m i t", t=PACK),
                )

        def quantize_w1(a, b):
            w1_q[a, b] = quantize("w1q%d%d" % (a, b), w1_bf[a, b], KP)

        def plain_reading(b):
            h2_bf = held("h2_bf%d" % b, [P, S * PACK], BF16)
            for jq in range(S // P):
                acc = bank("w4")
                js = slice(P * jq, P * (jq + 1))
                for a in range(PASSES):
                    for t in range(PACK):
                        c0 = KP * b + P * t
                        nc.tensor.matmul_mx(
                            out=acc[:, P * t : P * (t + 1)],
                            lhsT=w4_w[a][:, 2 * c0 : 2 * (c0 + P)].bitcast(FP4X4),
                            lhsT_scale=w4_sc[:, K * a + c0 : K * a + c0 + P],
                            rhs=new_w[a][:, js].bitcast(FP8X4),
                            rhs_scale=(new_sc, new_sc1)[a][:, js],
                            start=(a, t) == (0, 0),
                            stop=(a, t) == (PASSES - 1, PACK - 1),
                        )
                nc.vector.tensor_tensor(
                    out=h2_bf[:, KP * jq : KP * (jq + 1)].rearrange("p (j t) -> p j t", t=PACK),
                    in0=acc[:].rearrange("p (t j) -> p j t", t=PACK),
                    in1=g2[:, b : b + 1, :].to_broadcast([P, P, PACK]),
                    op=ALU.mult,
                )
            h2_q[b] = quantize("h2q%d" % b, h2_bf, S)

        def third_angle(b, jh):
            js = slice(JH * jh, JH * (jh + 1))
            s = held("s%d%d" % (b, jh), [P, PACK * JH], F32)
            sq = held("sq%d%d" % (b, jh), [P, PACK * JH], F32)
            sines[b, jh] = s, sq
            for pair in range(PACK // 2):
                acc = bank("w1")
                for a in range(PASSES):
                    words, scales = w1_q[a, b]
                    for ti in range(2):
                        cs = slice(P * (2 * pair + ti), P * (2 * pair + ti + 1))
                        nc.tensor.matmul_mx(
                            out=acc[:, JH * ti : JH * (ti + 1)],
                            lhsT=words[:, cs].bitcast(FP8X4),
                            lhsT_scale=scales[:, cs],
                            rhs=new_w[a][:, js].bitcast(FP8X4),
                            rhs_scale=new_sc[SC_ROWS * a : P, js],
                            start=(a, ti) == (0, 0),
                            stop=(a, ti) == (PASSES - 1, 1),
                        )
                cols = slice(BANK * pair, BANK * (pair + 1))
                nc.scalar.activation(out=s[:, cols], in_=acc[:], func=ACT.Sin, scale=-1.0 / 3.0)
                nc.scalar.activation(out=sq[:, cols], in_=s[:, cols], func=ACT.Square, scale=2.0)

        def sine_reading(b, jh):
            s, sq = sines[b, jh]
            u = held("u%d%d" % (b, jh), [P, PACK * JH], F32)
            for t in range(PACK):
                cols = slice(JH * t, JH * (t + 1))
                nc.vector.tensor_scalar(
                    out=u[:, cols], in0=sq[:, cols], scalar1=3.0, scalar2=g1[:, b, t : t + 1],
                    op0=ALU.subtract, op1=ALU.mult,
                )
            h1_bf = held("h1_bf%d%d" % (b, jh), [P, JH * PACK], BF16)
            nc.vector.tensor_tensor(
                out=h1_bf[:].rearrange("p (c n t) -> p c t n", n=LINE // 4, t=PACK),
                in0=s[:].rearrange("p (t c n) -> p c t n", t=PACK, n=LINE // 4),
                in1=u[:].rearrange("p (t c n) -> p c t n", t=PACK, n=LINE // 4),
                op=ALU.mult,
            )
            h1_q[b, jh] = quantize("h1q%d%d" % (b, jh), h1_bf, JH)

        def score(acc, tiles, h_q):
            width = BANK // len(tiles)
            for a in range(PASSES):
                words, scales = h_q[a]
                for ci, c in enumerate(tiles):
                    h, ch = divmod(c, TILES_PER_HALF)
                    cs = slice(P * ch, P * (ch + 1))
                    nc.tensor.matmul_mx(
                        out=acc[:, width * ci : width * (ci + 1)],
                        lhsT=known_w[a, h][:, cs].bitcast(FP8X4),
                        lhsT_scale=known_sc[h][SC_ROWS * a : P, cs],
                        rhs=words[:].bitcast(FP8X4),
                        rhs_scale=scales[:],
                        start=(a, ci) == (0, 0),
                        stop=(a, ci) == (PASSES - 1, len(tiles) - 1),
                    )

        def plain_scores(cp):
            e2[cp] = held("e2_%d" % cp, [P, 2, S], F32)
            for ci in range(2):
                acc = bank("w4")
                score(acc, [2 * cp + ci], h2_q)
                nc.scalar.copy(out=e2[cp][:, ci, :], in_=acc[:])

        def finish(cp, jh):
            js = slice(JH * jh, JH * (jh + 1))
            acc = bank(("w1", "w4")[jh])
            score(acc, [2 * cp, 2 * cp + 1], [h1_q[b, jh] for b in range(PASSES)])
            top = results.tile([P, 2, JH], F32, name="top")
            nc.vector.tensor_tensor(
                out=top[:], in0=acc[:].rearrange("p (c j) -> p c j", c=2), in1=e2[cp][:, :, js], op=ALU.max
            )
            res = results.tile([P, 2, JH], F32, name="res")
            for ci in range(2):
                c = 2 * cp + ci
                nc.scalar.activation(out=res[:, ci, :], in_=top[:, ci, :], func=ACT.Tanh, bias=neg_bar[:, c : c + 1])
            nc.sync.dma_start(
                out=out[2 * P * cp : 2 * P * (cp + 1), js].rearrange("(c p) j -> p c j", p=P), in_=res[:]
            )

        w4_w = [held("w4_w%d" % a, [P, 2 * K], U8) for a in range(PASSES)]
        for a in range(PASSES):
            nc.scalar.copy(
                out=w4_w[a][:].bitcast(U16).rearrange("p (b t o n) -> p b o t n", b=PASSES, t=PACK, n=LINE // 2),
                in_=w4_raw[:, 2 * K * a : 2 * K * (a + 1)]
                .bitcast(U16)
                .rearrange("p (b o n t) -> p b o t n", b=PASSES, t=PACK, n=LINE // 2),
            )
        w4_sc = held("w4_sc", [P, PASSES * K], U8)
        nc.vector.tensor_copy(
            out=w4_sc[:].rearrange("p (g t o n) -> p g o t n", g=PASSES * PASSES, t=PACK, n=LINE),
            in_=w4_sc_raw[:].rearrange("p (g o n t) -> p g o t n", g=PASSES * PASSES, t=PACK, n=LINE),
        )

        bar_t = bank("w1")
        nc.tensor.transpose(bar_t[:, 0:P], bar_rows[:], ident[:])
        neg_bar = held("neg_bar", [P, S2 // P], F32)
        nc.vector.tensor_scalar(out=neg_bar[:], in0=bar_t[:, 0 : S2 // P], scalar1=-1.0, scalar2=None, op0=ALU.mult)

        for a in range(PASSES):
            gather_new_words(a)
        for b in range(PASSES):
            for a in range(PASSES):
                round_w1(a, b)
                quantize_w1(a, b)
        for b in range(PASSES):
            plain_reading(b)
        for h in range(2):
            gather_known_scales(h)
        for a in range(PASSES):
            for h in range(2):
                gather_known_words(a, h)
        for b in range(PASSES):
            for jh in range(2):
                third_angle(b, jh)
        for cp in range(S2 // (2 * P)):
            plain_scores(cp)
        for b in range(PASSES):
            for jh in range(2):
                sine_reading(b, jh)
        for jh in range(2):
            for cp in range(S2 // (2 * P)):
                finish(cp, jh)
